import numpy as np
import ml_dtypes


def mxq(x, axis, fmt="e4m3"):
    dtype, down = {"e4m3": (ml_dtypes.float8_e4m3fn, 7), "e5m2": (ml_dtypes.float8_e5m2, 14)}[fmt]
    v = np.moveaxis(np.asarray(x, np.float32).astype(ml_dtypes.bfloat16).astype(np.float64), axis, -1)
    blocks = v.reshape(v.shape[:-1] + (-1, 32))
    amax = np.abs(blocks).max(-1, keepdims=True)
    byte = np.maximum(np.where(amax > 0, np.frexp(amax)[1] - 1 + 127, 0) - down, 1)
    scale = np.exp2(byte - 127.0)
    codes = (blocks / scale).astype(np.float32).astype(dtype).astype(np.float64)
    return np.moveaxis((codes * scale).reshape(v.shape), -1, axis)


WIDE = False


def mx_kscale(k):
    if not WIDE:
        return np.ones(k)
    levels = np.array([10, -10, 5, -5, 0])
    if k % 512:
        return np.exp2(np.random.permutation(np.resize(levels, k // 32))).repeat(32)
    a = np.empty((k // 512, 16))
    for p in range(k // 512):
        a[p, :8] = np.random.permutation(np.resize(levels, 8))
        for g in range(8):
            far = levels[np.abs(levels - a[p, g]) >= 10]
            a[p, g + 8] = far[np.random.randint(len(far))]
    return np.exp2(a.ravel()).repeat(32)


def f64(x):
    return np.asarray(x).astype(np.float64)


def striped(idx):
    return np.tile(idx.reshape(-1, 16).T, (8, 1)).astype(np.uint16)


def unstriped(offs):
    return offs[:16].T.reshape(-1).astype(np.int64)


def striped8(idx):
    return np.concatenate([x.reshape(-1, 16).T for x in idx]).astype(np.uint16)


def runs(offs, k):
    lists = np.stack([offs[16 * r : 16 * r + 16].T.reshape(-1) for r in range(8)]).astype(np.int64)
    return lists[np.arange(k) % 512 // 64]


def pack_weight(w):
    k, n = w.shape
    w = f64(np.asarray(w, np.float32).astype(ml_dtypes.bfloat16)).reshape(k // 32, 32, n)
    amax = np.abs(w).max(1)
    byte = np.clip(np.where(amax > 0, np.frexp(amax)[1] - 1 + 127 - 7, 1), 1, 254)
    scaled = (w * np.exp2(127.0 - byte)[:, None, :]).reshape(k, n).astype(np.float32)
    words = np.ascontiguousarray(scaled.reshape(k // 512, 128, 4, n).transpose(0, 1, 3, 2)).astype(ml_dtypes.float8_e4m3fn).view(np.uint8)
    return words, np.ascontiguousarray(byte.astype(np.uint8).reshape(k // 512, 16, n))


def unpack_weight(words, scales):
    g, p, n, _ = words.shape
    vals = np.ascontiguousarray(words).view(ml_dtypes.float8_e4m3fn).astype(np.float64) * np.repeat(np.exp2(scales.astype(np.float64) - 127.0), 8, axis=1)[..., None]
    return vals.transpose(0, 1, 3, 2).reshape(g * 512, n)


def sigmoid(v):
    return 1.0 / (1.0 + np.exp(-np.maximum(v, -700.0)))


K, T, S, G, H, C = 512, 1024, 256, 2048, 512, 512


def setup_inputs():
    n = np.random.standard_normal
    s = mx_kscale(K)[:, None]
    packed_xT = pack_weight(n((K, T)) * s)
    packed_dT = pack_weight(n((K, G)) / s)
    return {
        "x_words": packed_xT[0],
        "x_scales": packed_xT[1],
        "d_words": packed_dT[0],
        "d_scales": packed_dT[1],
        "sl": np.random.uniform(1.5, 3.0, (H, 1)).astype(np.float32),
        "th": (0.5 * n((H, 1))).astype(np.float32),
        "gs": (np.random.uniform(0.5, 1.5, (K, 1)) / s).astype(np.float32),
        "sl2": np.random.uniform(1.5, 2.5, (C, 1)).astype(np.float32),
        "lo": np.random.uniform(-1.2, -0.4, (C, 1)).astype(np.float32),
        "hi": np.random.uniform(0.4, 1.2, (C, 1)).astype(np.float32),
        "offs": striped(np.random.permutation(T)[:S]),
        "k1": striped8(np.random.randint(0, G, (8, H))),
        "n1": striped8(np.stack([np.random.permutation(S) for _ in range(8)])),
        "n2": striped8(np.stack([np.random.permutation(S) for _ in range(8)])),
        "cand": striped(np.random.permutation(T)[:C]),
        "n3": striped8(np.stack([np.random.permutation(S) for _ in range(8)])),
    }


def reference(x_words, x_scales, d_words, d_scales, sl, th, gs, sl2, lo, hi, offs, k1, n1, n2, cand, n3):
    x_cand = unpack_weight(x_words, x_scales)[:, unstriped(cand)]
    d_k1 = unpack_weight(d_words, d_scales)[np.arange(K)[:, None], runs(k1, K)]
    xq = unpack_weight(x_words, x_scales)[:, unstriped(offs)]
    h = 0.0625 * (d_k1.T @ xq)
    sg = sigmoid(f64(sl) * (h[np.arange(H)[:, None], runs(n1, H)] - f64(th)))
    z = f64(gs) * (1.5 * (h * (sg - (sg[np.arange(H)[:, None], runs(n2, H)]))))
    s = 0.0625 * ((x_cand.T @ mxq(z, 0, "e4m3")))
    sg2 = sigmoid(f64(sl2) * (s[np.arange(C)[:, None], runs(n3, C)] - f64(lo)))
    sg3 = sigmoid(f64(sl2) * (s[np.arange(C)[:, None], runs(n3, C)] - f64(hi)))
    return s * (sg2 - sg3)

@@ -1,0 +1,165 @@
+from contextlib import ExitStack
+
+import concourse.mybir as mybir
+
+F32 = mybir.dt.float32
+BF16 = mybir.dt.bfloat16
+I32 = mybir.dt.int32
+U32 = mybir.dt.uint32
+U16 = mybir.dt.uint16
+U8 = mybir.dt.uint8
+FP8X4 = mybir.dt.float8_e4m3fn_x4
+MULT = mybir.AluOpType.mult
+ADD = mybir.AluOpType.add
+SUB = mybir.AluOpType.subtract
+SIGMOID = mybir.ActivationFunctionType.Sigmoid
+COPY = mybir.ActivationFunctionType.Copy
+
+K, T, S, G, H, C = 512, 1024, 256, 2048, 512, 512
+P = 128
+PACK = 4
+HALF = S // 2
+FLOPS = 2 * K * H * S + 2 * K * C * S
+
+
+def tile_picked_pqcedbebd_none_p_kernel(tc, x_words, x_scales, d_words, d_scales, sl, th, gs, sl2, lo, hi, offs, k1, n1, n2, cand, n3, out):
+    nc = tc.nc
+    with ExitStack() as ctx:
+        keep = ctx.enter_context(tc.tile_pool(name="keep", bufs=1))
+        psum = ctx.enter_context(tc.psum_pool(name="psum", bufs=1))
+
+        def load_list(src, name):
+            t = keep.tile(list(src.shape), U16, name=name)
+            nc.sync.dma_start(t[:], src)
+            return t
+
+        def load_rows(src, name):
+            t = keep.tile([P, PACK], F32, name=name)
+            nc.gpsimd.dma_start(t[:], src.rearrange("(p t) o -> p (t o)", t=PACK))
+            return t
+
+        def load_words(src, width, name):
+            t = keep.tile([P, width], U32, name=name, align_bytes=64)
+            nc.sync.dma_start(t[:].bitcast(I32), src[0].rearrange("p n t -> p (n t)").bitcast(I32))
+            return t
+
+        d_bytes = keep.tile([P, G], U8, name="d_bytes", align_bytes=64)
+        x_bytes = keep.tile([P, T], U8, name="x_bytes", align_bytes=64)
+        nc.vector.memset(d_bytes[:].bitcast(I32), 0)
+        nc.vector.memset(x_bytes[:].bitcast(I32), 0)
+        h = [keep.tile([P, 2 * S], F32, name="h%d" % t) for t in range(PACK)]
+        for t in range(PACK):
+            nc.vector.memset(h[t][:, S:], 0.0)
+
+        k1_t = load_list(k1, "k1_t")
+        offs_t = load_list(offs, "offs_t")
+        cand_t = load_list(cand, "cand_t")
+        n1_t = load_list(n1, "n1_t")
+        n2_t = load_list(n2, "n2_t")
+        n3_t = load_list(n3, "n3_t")
+        nc.sync.dma_start(d_bytes[0:P:8, :].bitcast(I32), d_scales[0].bitcast(I32))
+        d_tab = load_words(d_words, G, "d_tab")
+        x_rows = x_scales[0].rearrange("(q a) c -> a q c", a=4)
+        for a in range(4):
+            nc.sync.dma_start(x_bytes[a:P:32, :].bitcast(I32), x_rows[a].bitcast(I32))
+        x_tab = load_words(x_words, T, "x_tab")
+
+        th_t = load_rows(th, "th_t")
+        sl_t = load_rows(sl, "sl_t")
+        gs_t = load_rows(gs, "gs_t")
+        sl2_t = load_rows(sl2, "sl2_t")
+        lo_t = load_rows(lo, "lo_t")
+        hi_t = load_rows(hi, "hi_t")
+
+        dk_bytes = keep.tile([P, H], U8, name="dk_bytes", tag="dk_bytes", align_bytes=64)
+        nc.vector.tensor_copy(dk_bytes[:], d_bytes[:].indirect(k1_t[:]))
+        w1_scales = keep.tile([P, H], U8, name="w1_scales", tag="lhs_scales", align_bytes=64)
+        nc.vector.tensor_copy(w1_scales[:].rearrange("p (t m) -> p t m", t=PACK), dk_bytes[:].rearrange("p (m t) -> p t m", t=PACK))
+        for a in range(1, 4):
+            nc.scalar.dma_start(w1_scales[a:P:32, :].bitcast(I32), w1_scales[8 * a : P : 32, :].bitcast(I32))
+
+        dk_words = keep.tile([P, H], U32, name="dk_words", align_bytes=64)
+        nc.vector.tensor_copy(dk_words[:], d_tab[:].indirect(k1_t[:]))
+        w1_words = keep.tile([P, H], U32, name="w1_words", tag="lhs_words", align_bytes=64)
+        nc.vector.tensor_copy(w1_words[:].rearrange("p (t m) -> p t m", t=PACK), dk_words[:].rearrange("p (m t) -> p t m", t=PACK))
+
+        xq_scales = keep.tile([P, S], U8, name="xq_scales", align_bytes=64)
+        nc.vector.tensor_copy(xq_scales[:], x_bytes[:].indirect(offs_t[:]))
+        xq_words = keep.tile([P, S], U32, name="xq_words", align_bytes=64)
+        nc.vector.tensor_copy(xq_words[:], x_tab[:].indirect(offs_t[:]))
+
+        bias1 = keep.tile([P, PACK], F32, name="bias1", tag="dk_bytes", align_bytes=64)
+        nc.vector.scalar_tensor_tensor(bias1[:], th_t[:], -1.0, sl_t[:], MULT, MULT)
+
+        for t in range(PACK):
+            acc = psum.tile([P, S], F32, name="acc_h%d" % t, tag="bank%d" % t)
+            cols = slice(t * P, (t + 1) * P)
+            nc.tensor.matmul_mx(out=acc[:], lhsT=w1_words[:, cols].bitcast(FP8X4), lhsT_scale=w1_scales[:, cols],
+                                rhs=xq_words[:].bitcast(FP8X4), rhs_scale=xq_scales[:], start=True, stop=True)
+            nc.vector.tensor_scalar(h[t][:, :S], acc[:], 0.0625, None, MULT)
+
+        w2_words = keep.tile([P, C], U32, name="w2_words", tag="lhs_words", align_bytes=64)
+        nc.vector.tensor_copy(w2_words[:].rearrange("p (t m) -> p m t", t=PACK), x_tab[:].indirect(cand_t[:]))
+        w2_scales = keep.tile([P, C], U8, name="w2_scales", tag="lhs_scales", align_bytes=64)
+        nc.vector.tensor_copy(w2_scales[:].rearrange("p (t m) -> p m t", t=PACK), x_bytes[:].indirect(cand_t[:]))
+
+        def cols_of(u):
+            return slice(u * HALF, (u + 1) * HALF)
+
+        def entries(lst, u):
+            return lst[:, u * HALF // 16 : (u + 1) * HALF // 16]
+
+        sg = []
+        for t in range(PACK):
+            sg_t = keep.tile([P, S], F32, name="sg%d" % t)
+            nc.scalar.activation(sg_t[:], h[t][:].indirect(n1_t[:]), SIGMOID,
+                                 bias=bias1[:, t : t + 1], scale=sl_t[:, t : t + 1])
+            sg.append(sg_t)
+
+        s = [keep.tile([P, 2 * S], F32, name="s%d" % t) for t in range(PACK)]
+        for u in range(2):
+            z32 = keep.tile([P, PACK, HALF], F32, name="z32_%d" % u)
+            diffs = [s[t][:, S + u * HALF : S + (u + 1) * HALF] for t in range(PACK)]
+            for step in range(PACK + 1):
+                if step < PACK:
+                    other = keep.tile([P, HALF], F32, name="sgn_%d_%d" % (u, step))
+                    nc.scalar.activation(other[:], sg[step][:].indirect(entries(n2_t, u)), COPY)
+                    nc.vector.tensor_tensor(diffs[step], sg[step][:, cols_of(u)], other[:], SUB)
+                if step > 0:
+                    t = step - 1
+                    nc.vector.scalar_tensor_tensor(z32[:, t, :], diffs[t], gs_t[:, t : t + 1], h[t][:, cols_of(u)], MULT, MULT)
+            z16 = keep.tile([P, HALF * PACK], BF16, name="z16_%d" % u, align_bytes=64)
+            nc.vector.tensor_scalar(z16[:].rearrange("p (c i t) -> p c t i", i=4, t=PACK),
+                                    z32[:].rearrange("p t (c i) -> p c t i", i=4), 1.5, None, MULT)
+            z_words = keep.tile([P, HALF], U32, name="z_words%d" % u, align_bytes=64)
+            z_scales = keep.tile([P, HALF], U8, name="z_scales%d" % u, align_bytes=64)
+            nc.vector.quantize_mx(out=z_words[:].bitcast(FP8X4), scales=z_scales[:], in_=z16[:])
+            for t in range(PACK):
+                acc = psum.tile([P, HALF], F32, name="acc_s%d_%d" % (u, t), tag="bank%d" % (PACK * (1 - u) + t))
+                cols = slice(t * P, (t + 1) * P)
+                nc.tensor.matmul_mx(out=acc[:], lhsT=w2_words[:, cols].bitcast(FP8X4), lhsT_scale=w2_scales[:, cols],
+                                    rhs=z_words[:].bitcast(FP8X4), rhs_scale=z_scales[:], start=True, stop=True)
+                if u == 0 or t == 0:
+                    nc.scalar.activation(s[t][:, cols_of(u)], acc[:], COPY, scale=0.0625)
+                else:
+                    nc.vector.tensor_scalar(s[t][:, cols_of(u)], acc[:], 0.0625, None, MULT)
+
+        neg_sl2 = keep.tile([P, PACK], F32, name="neg_sl2")
+        nc.gpsimd.tensor_scalar(neg_sl2[:], sl2_t[:], -1.0, 0.0, MULT, ADD)
+        bias2 = keep.tile([P, PACK], F32, name="bias2")
+        nc.gpsimd.tensor_tensor(bias2[:], lo_t[:], neg_sl2[:], MULT)
+        bias3 = keep.tile([P, PACK], F32, name="bias3")
+        nc.gpsimd.tensor_tensor(bias3[:], hi_t[:], neg_sl2[:], MULT)
+        out_rows = out.rearrange("(p t) c -> p t c", t=PACK)
+        pieces = [(t, 0, S) for t in range(PACK - 1)] + [(PACK - 1, 0, HALF), (PACK - 1, HALF, S)]
+        for t, c0, c1 in pieces:
+            sg2 = keep.tile([P, c1 - c0], F32, name="sg2_%d_%d" % (t, c0))
+            sg3 = keep.tile([P, c1 - c0], F32, name="sg3_%d_%d" % (t, c0))
+            for gate, bias in ((sg2, bias2), (sg3, bias3)):
+                nc.scalar.activation(gate[:], s[t][:].indirect(n3_t[:, c0 // 16 : c1 // 16]), SIGMOID,
+                                     bias=bias[:, t : t + 1], scale=sl2_t[:, t : t + 1])
+            band = keep.tile([P, c1 - c0], F32, name="band_%d_%d" % (t, c0))
+            nc.vector.tensor_tensor(band[:], sg2[:], sg3[:], SUB)
+            res = keep.tile([P, c1 - c0], F32, name="res_%d_%d" % (t, c0))
+            nc.vector.tensor_tensor(res[:], band[:], s[t][:, c0:c1], MULT)
+            nc.sync.dma_start(out_rows[:, t, c0:c1], res[:])

@@ -39,33 +39,36 @@ def tile_picked_pqcedbebd_none_p_kernel(tc, x_words, x_scales, d_words, d_scales
             return t
 
         def load_words(src, width, name):
-            t = keep.tile([P, width], U32, name=name, align_bytes=64)
+            t = keep.tile([P, width], U32, name=name, tag=name, align_bytes=64)
             nc.sync.dma_start(t[:].bitcast(I32), src[0].rearrange("p n t -> p (n t)").bitcast(I32))
             return t
 
         d_bytes = keep.tile([P, G], U8, name="d_bytes", align_bytes=64)
         x_bytes = keep.tile([P, T], U8, name="x_bytes", align_bytes=64)
-        nc.vector.memset(d_bytes[:].bitcast(I32), 0)
+        nc.gpsimd.memset(d_bytes[:].bitcast(I32), 0)
         nc.vector.memset(x_bytes[:].bitcast(I32), 0)
         h = [keep.tile([P, 2 * S], F32, name="h%d" % t) for t in range(PACK)]
         for t in range(PACK):
             nc.vector.memset(h[t][:, S:], 0.0)
+        s = [keep.tile([P, 2 * S], F32, name="s%d" % t) for t in range(PACK)]
+        for t in range(PACK):
+            nc.vector.memset(s[t][:, S + HALF :], 0.0)
 
         k1_t = load_list(k1, "k1_t")
         offs_t = load_list(offs, "offs_t")
-        cand_t = load_list(cand, "cand_t")
         n1_t = load_list(n1, "n1_t")
-        n2_t = load_list(n2, "n2_t")
-        n3_t = load_list(n3, "n3_t")
+        cand_t = load_list(cand, "cand_t")
         nc.sync.dma_start(d_bytes[0:P:8, :].bitcast(I32), d_scales[0].bitcast(I32))
         d_tab = load_words(d_words, G, "d_tab")
         x_rows = x_scales[0].rearrange("(q a) c -> a q c", a=4)
         for a in range(4):
             nc.sync.dma_start(x_bytes[a:P:32, :].bitcast(I32), x_rows[a].bitcast(I32))
         x_tab = load_words(x_words, T, "x_tab")
+        n2_t = load_list(n2, "n2_t")
+        n3_t = load_list(n3, "n3_t")
 
-        th_t = load_rows(th, "th_t")
         sl_t = load_rows(sl, "sl_t")
+        th_t = load_rows(th, "th_t")
         gs_t = load_rows(gs, "gs_t")
         sl2_t = load_rows(sl2, "sl2_t")
         lo_t = load_rows(lo, "lo_t")
@@ -76,27 +79,31 @@ def tile_picked_pqcedbebd_none_p_kernel(tc, x_words, x_scales, d_words, d_scales
         w1_scales = keep.tile([P, H], U8, name="w1_scales", tag="lhs_scales", align_bytes=64)
         nc.vector.tensor_copy(w1_scales[:].rearrange("p (t m) -> p t m", t=PACK), dk_bytes[:].rearrange("p (m t) -> p t m", t=PACK))
         for a in range(1, 4):
-            nc.scalar.dma_start(w1_scales[a:P:32, :].bitcast(I32), w1_scales[8 * a : P : 32, :].bitcast(I32))
+            nc.sync.dma_start(w1_scales[a:P:32, :].bitcast(I32), w1_scales[8 * a : P : 32, :].bitcast(I32))
 
-        dk_words = keep.tile([P, H], U32, name="dk_words", align_bytes=64)
+        dk_words = keep.tile([P, H], U32, name="dk_words", tag="dk_words", align_bytes=64)
         nc.vector.tensor_copy(dk_words[:], d_tab[:].indirect(k1_t[:]))
         w1_words = keep.tile([P, H], U32, name="w1_words", tag="lhs_words", align_bytes=64)
         nc.vector.tensor_copy(w1_words[:].rearrange("p (t m) -> p t m", t=PACK), dk_words[:].rearrange("p (m t) -> p t m", t=PACK))
 
-        xq_scales = keep.tile([P, S], U8, name="xq_scales", align_bytes=64)
+        xq_scales = keep.tile([P, S], U8, name="xq_scales", tag="d_tab", align_bytes=64)
         nc.vector.tensor_copy(xq_scales[:], x_bytes[:].indirect(offs_t[:]))
         xq_words = keep.tile([P, S], U32, name="xq_words", align_bytes=64)
         nc.vector.tensor_copy(xq_words[:], x_tab[:].indirect(offs_t[:]))
 
-        bias1 = keep.tile([P, PACK], F32, name="bias1", tag="dk_bytes", align_bytes=64)
+        bias1 = keep.tile([P, PACK], F32, name="bias1", tag="dk_words", align_bytes=64)
         nc.vector.scalar_tensor_tensor(bias1[:], th_t[:], -1.0, sl_t[:], MULT, MULT)
 
+        gs15 = keep.tile([P, PACK], F32, name="gs15")
+        nc.gpsimd.tensor_scalar(gs15[:], gs_t[:], 1.5, 0.0, MULT, ADD)
+        gh = keep.tile([P, PACK, S], F32, name="gh")
         for t in range(PACK):
             acc = psum.tile([P, S], F32, name="acc_h%d" % t, tag="bank%d" % t)
             cols = slice(t * P, (t + 1) * P)
             nc.tensor.matmul_mx(out=acc[:], lhsT=w1_words[:, cols].bitcast(FP8X4), lhsT_scale=w1_scales[:, cols],
                                 rhs=xq_words[:].bitcast(FP8X4), rhs_scale=xq_scales[:], start=True, stop=True)
             nc.vector.tensor_scalar(h[t][:, :S], acc[:], 0.0625, None, MULT)
+            nc.gpsimd.tensor_scalar(gh[:, t, :], h[t][:, :S], gs15[:, t : t + 1], 0.0, MULT, ADD)
 
         w2_words = keep.tile([P, C], U32, name="w2_words", tag="lhs_words", align_bytes=64)
         nc.vector.tensor_copy(w2_words[:].rearrange("p (t m) -> p m t", t=PACK), x_tab[:].indirect(cand_t[:]))
@@ -109,28 +116,32 @@ def tile_picked_pqcedbebd_none_p_kernel(tc, x_words, x_scales, d_words, d_scales
         def entries(lst, u):
             return lst[:, u * HALF // 16 : (u + 1) * HALF // 16]
 
-        sg = []
-        for t in range(PACK):
-            sg_t = keep.tile([P, S], F32, name="sg%d" % t)
-            nc.scalar.activation(sg_t[:], h[t][:].indirect(n1_t[:]), SIGMOID,
-                                 bias=bias1[:, t : t + 1], scale=sl_t[:, t : t + 1])
-            sg.append(sg_t)
+        sg = [keep.tile([P, S], F32, name="sg%d" % t) for t in range(PACK)]
+        late = keep.tile([P, PACK, HALF], F32, name="late", tag="dk_words", align_bytes=64)
+        fetched = [[s[t][:, S : S + HALF] for t in range(PACK)], [late[:, t, :] for t in range(PACK)]]
+        diff = keep.tile([P, PACK, S], F32, name="diff")
 
-        s = [keep.tile([P, 2 * S], F32, name="s%d" % t) for t in range(PACK)]
+        def fetch_n2(t, u):
+            nc.scalar.activation(fetched[u][t], sg[t][:].indirect(entries(n2_t, u)), COPY)
+
+        def subtract(t, u):
+            nc.vector.tensor_tensor(diff[:, t, cols_of(u)], sg[t][:, cols_of(u)], fetched[u][t], SUB)
+
+        for t in range(PACK):
+            nc.scalar.activation(sg[t][:], h[t][:].indirect(n1_t[:]), SIGMOID,
+                                 bias=bias1[:, t : t + 1], scale=sl_t[:, t : t + 1])
+            if t > 0:
+                fetch_n2(t - 1, 0)
+                subtract(t - 1, 0)
+
         for u in range(2):
-            z32 = keep.tile([P, PACK, HALF], F32, name="z32_%d" % u)
-            diffs = [s[t][:, S + u * HALF : S + (u + 1) * HALF] for t in range(PACK)]
-            for step in range(PACK + 1):
-                if step < PACK:
-                    other = keep.tile([P, HALF], F32, name="sgn_%d_%d" % (u, step))
-                    nc.scalar.activation(other[:], sg[step][:].indirect(entries(n2_t, u)), COPY)
-                    nc.vector.tensor_tensor(diffs[step], sg[step][:, cols_of(u)], other[:], SUB)
-                if step > 0:
-                    t = step - 1
-                    nc.vector.scalar_tensor_tensor(z32[:, t, :], diffs[t], gs_t[:, t : t + 1], h[t][:, cols_of(u)], MULT, MULT)
+            for t in range(PACK - 1 if u == 0 else 0, PACK):
+                fetch_n2(t, u)
+                subtract(t, u)
             z16 = keep.tile([P, HALF * PACK], BF16, name="z16_%d" % u, align_bytes=64)
-            nc.vector.tensor_scalar(z16[:].rearrange("p (c i t) -> p c t i", i=4, t=PACK),
-                                    z32[:].rearrange("p t (c i) -> p c t i", i=4), 1.5, None, MULT)
+            nc.vector.tensor_tensor(z16[:].rearrange("p (c i t) -> p c t i", i=4, t=PACK),
+                                    diff[:, :, cols_of(u)].rearrange("p t (c i) -> p c t i", i=4),
+                                    gh[:, :, cols_of(u)].rearrange("p t (c i) -> p c t i", i=4), MULT)
             z_words = keep.tile([P, HALF], U32, name="z_words%d" % u, align_bytes=64)
             z_scales = keep.tile([P, HALF], U8, name="z_scales%d" % u, align_bytes=64)
             nc.vector.quantize_mx(out=z_words[:].bitcast(FP8X4), scales=z_scales[:], in_=z16[:])

@@ -33,10 +33,9 @@ def tile_picked_pqcedbebd_none_p_kernel(tc, x_words, x_scales, d_words, d_scales
             nc.sync.dma_start(t[:], src)
             return t
 
-        def load_rows(src, name):
-            t = keep.tile([P, PACK], F32, name=name)
-            nc.gpsimd.dma_start(t[:], src.rearrange("(p t) o -> p (t o)", t=PACK))
-            return t
+        def load_rows(src, dst):
+            nc.sync.dma_start(dst, src.rearrange("(p t) o -> p (t o)", t=PACK))
+            return dst
 
         def load_words(src, width, name):
             t = keep.tile([P, width], U32, name=name, tag=name, align_bytes=64)
@@ -63,16 +62,11 @@ def tile_picked_pqcedbebd_none_p_kernel(tc, x_words, x_scales, d_words, d_scales
         x_rows = x_scales[0].rearrange("(q a) c -> a q c", a=4)
         for a in range(4):
             nc.sync.dma_start(x_bytes[a:P:32, :].bitcast(I32), x_rows[a].bitcast(I32))
+        sl_t = load_rows(sl, keep.tile([P, PACK], F32, name="sl_rows")[:])
+        th_t = load_rows(th, keep.tile([P, PACK], F32, name="th_rows")[:])
         x_tab = load_words(x_words, T, "x_tab")
         n2_t = load_list(n2, "n2_t")
         n3_t = load_list(n3, "n3_t")
-
-        sl_t = load_rows(sl, "sl_t")
-        th_t = load_rows(th, "th_t")
-        gs_t = load_rows(gs, "gs_t")
-        sl2_t = load_rows(sl2, "sl2_t")
-        lo_t = load_rows(lo, "lo_t")
-        hi_t = load_rows(hi, "hi_t")
 
         dk_bytes = keep.tile([P, H], U8, name="dk_bytes", tag="dk_bytes", align_bytes=64)
         nc.vector.tensor_copy(dk_bytes[:], d_bytes[:].indirect(k1_t[:]))
@@ -81,10 +75,15 @@ def tile_picked_pqcedbebd_none_p_kernel(tc, x_words, x_scales, d_words, d_scales
         for a in range(1, 4):
             nc.sync.dma_start(w1_scales[a:P:32, :].bitcast(I32), w1_scales[8 * a : P : 32, :].bitcast(I32))
 
+        later_rows = keep.tile([P, 4, 8], F32, name="later_rows", tag="dk_bytes", align_bytes=64)
+        gs_t, sl2_t, lo_t, hi_t = [load_rows(src, later_rows[:, i, 0:PACK]) for i, src in enumerate((gs, sl2, lo, hi))]
+
         dk_words = keep.tile([P, H], U32, name="dk_words", tag="dk_words", align_bytes=64)
         nc.vector.tensor_copy(dk_words[:], d_tab[:].indirect(k1_t[:]))
         w1_words = keep.tile([P, H], U32, name="w1_words", tag="lhs_words", align_bytes=64)
-        nc.vector.tensor_copy(w1_words[:].rearrange("p (t m) -> p t m", t=PACK), dk_words[:].rearrange("p (m t) -> p t m", t=PACK))
+        dealt = w1_words[:].rearrange("p (t m) -> p t m", t=PACK)
+        picked = dk_words[:].rearrange("p (m t) -> p t m", t=PACK)
+        nc.vector.tensor_copy(dealt, picked)
 
         xq_scales = keep.tile([P, S], U8, name="xq_scales", tag="d_tab", align_bytes=64)
         nc.vector.tensor_copy(xq_scales[:], x_bytes[:].indirect(offs_t[:]))
@@ -92,10 +91,10 @@ def tile_picked_pqcedbebd_none_p_kernel(tc, x_words, x_scales, d_words, d_scales
         nc.vector.tensor_copy(xq_words[:], x_tab[:].indirect(offs_t[:]))
 
         bias1 = keep.tile([P, PACK], F32, name="bias1", tag="dk_words", align_bytes=64)
-        nc.vector.scalar_tensor_tensor(bias1[:], th_t[:], -1.0, sl_t[:], MULT, MULT)
+        nc.vector.scalar_tensor_tensor(bias1[:], th_t, -1.0, sl_t, MULT, MULT)
 
         gs15 = keep.tile([P, PACK], F32, name="gs15")
-        nc.gpsimd.tensor_scalar(gs15[:], gs_t[:], 1.5, 0.0, MULT, ADD)
+        nc.gpsimd.tensor_scalar(gs15[:], gs_t, 1.5, 0.0, MULT, ADD)
         gh = keep.tile([P, PACK, S], F32, name="gh")
         for t in range(PACK):
             acc = psum.tile([P, S], F32, name="acc_h%d" % t, tag="bank%d" % t)
@@ -156,11 +155,11 @@ def tile_picked_pqcedbebd_none_p_kernel(tc, x_words, x_scales, d_words, d_scales
                     nc.vector.tensor_scalar(s[t][:, cols_of(u)], acc[:], 0.0625, None, MULT)
 
         neg_sl2 = keep.tile([P, PACK], F32, name="neg_sl2")
-        nc.gpsimd.tensor_scalar(neg_sl2[:], sl2_t[:], -1.0, 0.0, MULT, ADD)
+        nc.gpsimd.tensor_scalar(neg_sl2[:], sl2_t, -1.0, 0.0, MULT, ADD)
         bias2 = keep.tile([P, PACK], F32, name="bias2")
-        nc.gpsimd.tensor_tensor(bias2[:], lo_t[:], neg_sl2[:], MULT)
+        nc.gpsimd.tensor_tensor(bias2[:], lo_t, neg_sl2[:], MULT)
         bias3 = keep.tile([P, PACK], F32, name="bias3")
-        nc.gpsimd.tensor_tensor(bias3[:], hi_t[:], neg_sl2[:], MULT)
+        nc.gpsimd.tensor_tensor(bias3[:], hi_t, neg_sl2[:], MULT)
         out_rows = out.rearrange("(p t) c -> p t c", t=PACK)
         pieces = [(t, 0, S) for t in range(PACK - 1)] + [(PACK - 1, 0, HALF), (PACK - 1, HALF, S)]
         for t, c0, c1 in pieces:

from contextlib import ExitStack

import concourse.mybir as mybir

F32 = mybir.dt.float32
BF16 = mybir.dt.bfloat16
I32 = mybir.dt.int32
U32 = mybir.dt.uint32
U16 = mybir.dt.uint16
U8 = mybir.dt.uint8
FP8X4 = mybir.dt.float8_e4m3fn_x4
MULT = mybir.AluOpType.mult
ADD = mybir.AluOpType.add
SUB = mybir.AluOpType.subtract
SIGMOID = mybir.ActivationFunctionType.Sigmoid
COPY = mybir.ActivationFunctionType.Copy

K, T, S, G, H, C = 512, 1024, 256, 2048, 512, 512
P = 128
PACK = 4
HALF = S // 2
FLOPS = 2 * K * H * S + 2 * K * C * S


def tile_picked_pqcedbebd_none_p_kernel(tc, x_words, x_scales, d_words, d_scales, sl, th, gs, sl2, lo, hi, offs, k1, n1, n2, cand, n3, out):
    nc = tc.nc
    with ExitStack() as ctx:
        keep = ctx.enter_context(tc.tile_pool(name="keep", bufs=1))
        psum = ctx.enter_context(tc.psum_pool(name="psum", bufs=1))

        def load_list(src, name):
            t = keep.tile(list(src.shape), U16, name=name)
            nc.sync.dma_start(t[:], src)
            return t

        def load_rows(src, dst):
            nc.sync.dma_start(dst, src.rearrange("(p t) o -> p (t o)", t=PACK))
            return dst

        def load_words(src, width, name):
            t = keep.tile([P, width], U32, name=name, tag=name, align_bytes=64)
            nc.sync.dma_start(t[:].bitcast(I32), src[0].rearrange("p n t -> p (n t)").bitcast(I32))
            return t

        d_bytes = keep.tile([P, G], U8, name="d_bytes", align_bytes=64)
        x_bytes = keep.tile([P, T], U8, name="x_bytes", align_bytes=64)
        nc.gpsimd.memset(d_bytes[:].bitcast(I32), 0)
        nc.vector.memset(x_bytes[:].bitcast(I32), 0)
        h = [keep.tile([P, 2 * S], F32, name="h%d" % t) for t in range(PACK)]
        for t in range(PACK):
            nc.vector.memset(h[t][:, S:], 0.0)
        s = [keep.tile([P, 2 * S], F32, name="s%d" % t) for t in range(PACK)]
        for t in range(PACK):
            nc.vector.memset(s[t][:, S + HALF :], 0.0)

        k1_t = load_list(k1, "k1_t")
        offs_t = load_list(offs, "offs_t")
        n1_t = load_list(n1, "n1_t")
        cand_t = load_list(cand, "cand_t")
        nc.sync.dma_start(d_bytes[0:P:8, :].bitcast(I32), d_scales[0].bitcast(I32))
        d_tab = load_words(d_words, G, "d_tab")
        x_rows = x_scales[0].rearrange("(q a) c -> a q c", a=4)
        for a in range(4):
            nc.sync.dma_start(x_bytes[a:P:32, :].bitcast(I32), x_rows[a].bitcast(I32))
        sl_t = load_rows(sl, keep.tile([P, PACK], F32, name="sl_rows")[:])
        th_t = load_rows(th, keep.tile([P, PACK], F32, name="th_rows")[:])
        x_tab = load_words(x_words, T, "x_tab")
        n2_t = load_list(n2, "n2_t")
        n3_t = load_list(n3, "n3_t")

        dk_bytes = keep.tile([P, H], U8, name="dk_bytes", tag="dk_bytes", align_bytes=64)
        nc.vector.tensor_copy(dk_bytes[:], d_bytes[:].indirect(k1_t[:]))
        w1_scales = keep.tile([P, H], U8, name="w1_scales", tag="lhs_scales", align_bytes=64)
        nc.vector.tensor_copy(w1_scales[:].rearrange("p (t m) -> p t m", t=PACK), dk_bytes[:].rearrange("p (m t) -> p t m", t=PACK))
        for a in range(1, 4):
            nc.sync.dma_start(w1_scales[a:P:32, :].bitcast(I32), w1_scales[8 * a : P : 32, :].bitcast(I32))

        later_rows = keep.tile([P, 4, 8], F32, name="later_rows", tag="dk_bytes", align_bytes=64)
        gs_t, sl2_t, lo_t, hi_t = [load_rows(src, later_rows[:, i, 0:PACK]) for i, src in enumerate((gs, sl2, lo, hi))]

        dk_words = keep.tile([P, H], U32, name="dk_words", tag="dk_words", align_bytes=64)
        nc.vector.tensor_copy(dk_words[:], d_tab[:].indirect(k1_t[:]))
        w1_words = keep.tile([P, H], U32, name="w1_words", tag="lhs_words", align_bytes=64)
        dealt = w1_words[:].rearrange("p (t m) -> p t m", t=PACK)
        picked = dk_words[:].rearrange("p (m t) -> p t m", t=PACK)
        nc.vector.tensor_copy(dealt, picked)

        xq_scales = keep.tile([P, S], U8, name="xq_scales", tag="d_tab", align_bytes=64)
        nc.vector.tensor_copy(xq_scales[:], x_bytes[:].indirect(offs_t[:]))
        xq_words = keep.tile([P, S], U32, name="xq_words", align_bytes=64)
        nc.vector.tensor_copy(xq_words[:], x_tab[:].indirect(offs_t[:]))

        bias1 = keep.tile([P, PACK], F32, name="bias1", tag="dk_words", align_bytes=64)
        nc.vector.scalar_tensor_tensor(bias1[:], th_t, -1.0, sl_t, MULT, MULT)

        gs15 = keep.tile([P, PACK], F32, name="gs15")
        nc.gpsimd.tensor_scalar(gs15[:], gs_t, 1.5, 0.0, MULT, ADD)
        gh = keep.tile([P, PACK, S], F32, name="gh")
        for t in range(PACK):
            acc = psum.tile([P, S], F32, name="acc_h%d" % t, tag="bank%d" % t)
            cols = slice(t * P, (t + 1) * P)
            nc.tensor.matmul_mx(out=acc[:], lhsT=w1_words[:, cols].bitcast(FP8X4), lhsT_scale=w1_scales[:, cols],
                                rhs=xq_words[:].bitcast(FP8X4), rhs_scale=xq_scales[:], start=True, stop=True)
            nc.vector.tensor_scalar(h[t][:, :S], acc[:], 0.0625, None, MULT)
            nc.gpsimd.tensor_scalar(gh[:, t, :], h[t][:, :S], gs15[:, t : t + 1], 0.0, MULT, ADD)

        w2_words = keep.tile([P, C], U32, name="w2_words", tag="lhs_words", align_bytes=64)
        nc.vector.tensor_copy(w2_words[:].rearrange("p (t m) -> p m t", t=PACK), x_tab[:].indirect(cand_t[:]))
        w2_scales = keep.tile([P, C], U8, name="w2_scales", tag="lhs_scales", align_bytes=64)
        nc.vector.tensor_copy(w2_scales[:].rearrange("p (t m) -> p m t", t=PACK), x_bytes[:].indirect(cand_t[:]))

        def cols_of(u):
            return slice(u * HALF, (u + 1) * HALF)

        def entries(lst, u):
            return lst[:, u * HALF // 16 : (u + 1) * HALF // 16]

        sg = [keep.tile([P, S], F32, name="sg%d" % t) for t in range(PACK)]
        late = keep.tile([P, PACK, HALF], F32, name="late", tag="dk_words", align_bytes=64)
        fetched = [[s[t][:, S : S + HALF] for t in range(PACK)], [late[:, t, :] for t in range(PACK)]]
        diff = keep.tile([P, PACK, S], F32, name="diff")

        def fetch_n2(t, u):
            nc.scalar.activation(fetched[u][t], sg[t][:].indirect(entries(n2_t, u)), COPY)

        def subtract(t, u):
            nc.vector.tensor_tensor(diff[:, t, cols_of(u)], sg[t][:, cols_of(u)], fetched[u][t], SUB)

        for t in range(PACK):
            nc.scalar.activation(sg[t][:], h[t][:].indirect(n1_t[:]), SIGMOID,
                                 bias=bias1[:, t : t + 1], scale=sl_t[:, t : t + 1])
            if t > 0:
                fetch_n2(t - 1, 0)
                subtract(t - 1, 0)

        for u in range(2):
            for t in range(PACK - 1 if u == 0 else 0, PACK):
                fetch_n2(t, u)
                subtract(t, u)
            z16 = keep.tile([P, HALF * PACK], BF16, name="z16_%d" % u, align_bytes=64)
            nc.vector.tensor_tensor(z16[:].rearrange("p (c i t) -> p c t i", i=4, t=PACK),
                                    diff[:, :, cols_of(u)].rearrange("p t (c i) -> p c t i", i=4),
                                    gh[:, :, cols_of(u)].rearrange("p t (c i) -> p c t i", i=4), MULT)
            z_words = keep.tile([P, HALF], U32, name="z_words%d" % u, align_bytes=64)
            z_scales = keep.tile([P, HALF], U8, name="z_scales%d" % u, align_bytes=64)
            nc.vector.quantize_mx(out=z_words[:].bitcast(FP8X4), scales=z_scales[:], in_=z16[:])
            for t in range(PACK):
                acc = psum.tile([P, HALF], F32, name="acc_s%d_%d" % (u, t), tag="bank%d" % (PACK * (1 - u) + t))
                cols = slice(t * P, (t + 1) * P)
                nc.tensor.matmul_mx(out=acc[:], lhsT=w2_words[:, cols].bitcast(FP8X4), lhsT_scale=w2_scales[:, cols],
                                    rhs=z_words[:].bitcast(FP8X4), rhs_scale=z_scales[:], start=True, stop=True)
                if u == 0 or t == 0:
                    nc.scalar.activation(s[t][:, cols_of(u)], acc[:], COPY, scale=0.0625)
                else:
                    nc.vector.tensor_scalar(s[t][:, cols_of(u)], acc[:], 0.0625, None, MULT)

        neg_sl2 = keep.tile([P, PACK], F32, name="neg_sl2")
        nc.gpsimd.tensor_scalar(neg_sl2[:], sl2_t, -1.0, 0.0, MULT, ADD)
        bias2 = keep.tile([P, PACK], F32, name="bias2")
        nc.gpsimd.tensor_tensor(bias2[:], lo_t, neg_sl2[:], MULT)
        bias3 = keep.tile([P, PACK], F32, name="bias3")
        nc.gpsimd.tensor_tensor(bias3[:], hi_t, neg_sl2[:], MULT)
        out_rows = out.rearrange("(p t) c -> p t c", t=PACK)
        pieces = [(t, 0, S) for t in range(PACK - 1)] + [(PACK - 1, 0, HALF), (PACK - 1, HALF, S)]
        for t, c0, c1 in pieces:
            sg2 = keep.tile([P, c1 - c0], F32, name="sg2_%d_%d" % (t, c0))
            sg3 = keep.tile([P, c1 - c0], F32, name="sg3_%d_%d" % (t, c0))
            for gate, bias in ((sg2, bias2), (sg3, bias3)):
                nc.scalar.activation(gate[:], s[t][:].indirect(n3_t[:, c0 // 16 : c1 // 16]), SIGMOID,
                                     bias=bias[:, t : t + 1], scale=sl2_t[:, t : t + 1])
            band = keep.tile([P, c1 - c0], F32, name="band_%d_%d" % (t, c0))
            nc.vector.tensor_tensor(band[:], sg2[:], sg3[:], SUB)
            res = keep.tile([P, c1 - c0], F32, name="res_%d_%d" % (t, c0))
            nc.vector.tensor_tensor(res[:], band[:], s[t][:, c0:c1], MULT)
            nc.sync.dma_start(out_rows[:, t, c0:c1], res[:])
